import numpy as np, ml_dtypes
CORES = [78,86,94,102,110,118]
N = 6
TOK, CAP, FF = 64, 32, 8
def entries(a): return a.T.reshape(-1)
def pack(v, P): return np.ascontiguousarray(np.asarray(v, np.int32).reshape(-1, P).T)
def lists(rng, how):
    E = rng.integers(0, N, (N, TOK))
    if how == "hot": E[:] = rng.integers(N)
    if how == "none": E = (int(rng.integers(N)) + 1 + rng.integers(0, N - 1, (N, TOK))) % N
    if how == "skew": E = np.where(rng.random((N, TOK)) < 0.7, rng.integers(0, N, (N, 1)), E)
    if how == "even": E = np.stack([rng.permutation(np.arange(TOK) % N) for r in range(N)])
    if how == "own": E = np.repeat(np.arange(N).reshape(N, 1), TOK, axis=1)
    return {"ex": np.stack([pack(E[r], 16) for r in range(N)]), "pos": np.stack([pack(p, 16) for p in np.stack([np.array([np.sum(E[r, :t] == E[r, t]) for t in range(TOK)]) for r in range(N)])])}
def setup_inputs(rng):
    return dict({"x": rng.standard_normal((N, 128, TOK), dtype=np.float32).astype(ml_dtypes.bfloat16), "w1": (rng.standard_normal((N, 128, FF * 128), dtype=np.float32) / 8).astype(ml_dtypes.bfloat16), "w2": (rng.standard_normal((N, 128, FF * 128), dtype=np.float32) / 16).astype(ml_dtypes.bfloat16)}, **lists(rng, "uniform"))
def setup_inputs_even(rng):
    d = setup_inputs(rng); d.update(lists(rng, "even"))
    for k in ("x",): d[k] = (d[k].astype(np.float32) * 1024.0).astype(d[k].dtype)
    return d
def setup_inputs_hot(rng):
    d = setup_inputs(rng); d.update(lists(rng, "hot"))
    for k in ("x",): d[k] = (d[k].astype(np.float32) * (1 / 1024.0)).astype(d[k].dtype)
    return d
def setup_inputs_none(rng):
    d = setup_inputs(rng); d.update(lists(rng, "none"))
    return d
def setup_inputs_own(rng):
    d = setup_inputs(rng); d.update(lists(rng, "own"))
    return d
def setup_inputs_skew(rng):
    d = setup_inputs(rng); d.update(lists(rng, "skew"))
    return d
def check_inputs(x):
    bad = []
    if x["ex"].min() < 0 or x["ex"].max() >= N: bad.append("ex out of range")
    E = np.stack([entries(a) for a in x["ex"]])
    if not np.array_equal(np.stack([entries(a) for a in x["pos"]]), np.stack([np.array([np.sum(E[r, :t] == E[r, t]) for t in range(TOK)]) for r in range(N)])): bad.append("pos isn't the place")
    return bad
def reference(x, w1, w2, ex, pos):
    X, W1, W2 = x.astype(np.float64), w1.astype(np.float64), w2.astype(np.float64)
    y = np.zeros((N, 128, TOK))
    for r in range(N):
        E = entries(ex[r]); place = np.array([np.sum(E[:t] == E[t]) for t in range(TOK)])
        for k in range(N):
            m = (E == k) & (place < CAP)
            y[r][:, m] = sum(W2[k][:, 128 * f:128 * f + 128].T @ np.maximum(W1[k][:, 128 * f:128 * f + 128].T @ X[r][:, m], 0.0) for f in range(FF))
    return {"y": y.astype(ml_dtypes.bfloat16)}

@@ -1,0 +1,188 @@
+from concourse.bass import DstId, RemoteDMATransfer
+from concourse.mybir import AluOpType, ActivationFunctionType
+
+N, TOK, CAP, FF, D = 6, 64, 32, 8, 128
+STRIDE = 2 * CAP
+WIN = N * STRIDE
+WAVES = [[8], [4, 4], [4, 4]]
+OWN_GROUP = 0
+NG = len(WAVES)
+COLS = N * CAP
+HB, AHEAD = 4, 3
+
+SCRATCH = {
+    "tab": ("sbuf", [32, 4], "int32"),
+    "tabb": ("sbuf", [32, 4], "bfloat16"),
+    "sel": ("sbuf", [32, D], "bfloat16"),
+    "off": ("sbuf", [D, 4], "uint16"),
+    "xs": ("sbuf", [D, TOK], "bfloat16"),
+    "slots": ("sbuf", [D, WIN], "bfloat16"),
+    "xin": ("sbuf", [D, COLS], "bfloat16"),
+    "w1s": ("sbuf", [D, FF * D], "bfloat16"),
+    "w2s": ("sbuf", [D, FF * D], "bfloat16"),
+    "hs": ("sbuf", [D, FF * COLS], "bfloat16"),
+    "yo": ("sbuf", [D, COLS], "bfloat16"),
+    "back": ("sbuf", [D, WIN], "bfloat16"),
+    "ys": ("sbuf", [D, TOK], "bfloat16"),
+}
+for _b in range(8):
+    SCRATCH["p%d" % _b] = ("psum", [D, 512], "float32")
+
+SEMAPHORES = ["ldtab", "ldx", "ldw1", "ldw2", "mssel", "sel1", "selok", "msslots", "msback", "cv", "mmoff", "offok",
+              "sc", "owncp", "evown", "ret", "gat", "st", "lsem"]
+for _g in range(NG):
+    SEMAPHORES += ["arr%d" % _g, "l2_%d" % _g, "ev%d" % _g]
+    for _f in range(FF):
+        SEMAPHORES += ["l1_%d_%d" % (_g, _f), "rl_%d_%d" % (_g, _f)]
+
+
+def plan(cores, topo):
+    n = len(cores)
+
+    def hops(d):
+        worst = 1
+        for r in range(n):
+            a, b = topo.chip(cores[r]), topo.chip(cores[(r + d) % n])
+            if not (topo.mates(a, b) or topo.same_plane(a, b)):
+                worst = 2
+        return worst
+
+    order = sorted(range(1, n), key=lambda d: (-hops(d), d))
+    groups, i, col = [], 0, 0
+    for gi, shape in enumerate(WAVES):
+        c0, own = col, None
+        if gi == OWN_GROUP:
+            own = col
+            col += CAP
+        mem = []
+        for ne in shape:
+            mem.append((order[i], ne, col))
+            i += 1
+            col += CAP
+        groups.append({"c0": c0, "n": col - c0, "own": own, "mem": mem})
+    return groups
+
+
+def send(g, core, topo, items, local_sem):
+    used, trs = 0, []
+    for dst, ne, src, land, rsem in items:
+        if not topo.may_write(core, dst):
+            raise ValueError("no way from %d to %d" % (core, dst))
+        allowed = topo.mask(core, dst)
+        free = [b for b in range(allowed.bit_length()) if (allowed >> b) & 1 and not (used >> b) & 1]
+        m = 0
+        for b in free[:ne]:
+            m |= 1 << b
+        used |= m
+        rid, pid, ring = topo.addr(dst)
+        trs.append((rid, pid, m, src, land, rsem))
+    if len(trs) == 1:
+        rid, pid, m, src, land, rsem = trs[0]
+        g.remote_dma(land, src, rsem, local_sem, pid, rid, m)
+    else:
+        g.remote_dma_fused([RemoteDMATransfer(dst_ids=[DstId(rid=rid, pnc=pid)], dma_engine_mask=m, remote_sem=rsem,
+                                              src=src, dst=land) for rid, pid, m, src, land, rsem in trs],
+                           local_sem=local_sem)
+
+
+def rank_program(g, core, T, topo):
+    me = T.rank_of(core)
+    if me is None:
+        return
+    S, cores = T.sem, T.cores
+    v, pe, act, sy = g.vector, g.tensor, g.scalar, g.sync
+    groups = plan(cores, topo)
+    mine = me * STRIDE
+    hbank = [T["p%d" % b] for b in range(HB)]
+    ybank = [T["p%d" % (HB + gi)] for gi in range(NG)]
+    offp = T.p7
+
+    sy.dma_start(T.tab[0:16, :], T.ex[:]).then_inc(S.ldtab, 16)
+    act.dma_start(T.tab[16:32, :], T.pos[:]).then_inc(S.ldtab, 16)
+    sy.dma_start(T.xs[:], T.x[:]).then_inc(S.ldx, 16)
+    sy.dma_start(T.w1s[:], T.w1[:]).then_inc(S.ldw1, 16)
+    sy.dma_start(T.w2s[:], T.w2[:]).then_inc(S.ldw2, 16)
+
+    v.memset(T.sel[:], 64.0).then_inc(S.mssel, 1)
+    v.memset(T.slots[:], 0.0).then_inc(S.msslots, 1)
+    for k in range(N):
+        v.memset(T.back[:, k * STRIDE + CAP:(k + 1) * STRIDE], 0.0).then_inc(S.msback, 1)
+    g.wait_ge(S.mssel, 1)
+    g.affine_select(T.sel[:], T.sel[:], [[0, D // 16], [-1, 16]], AluOpType.is_equal, 0.0, 0, 1).then_inc(S.sel1, 1)
+    g.wait_ge(S.sel1, 1)
+    g.affine_select(T.sel[:], T.sel[:], [[0, D // 16], [-1, 16]], AluOpType.not_equal, 1.0, -16, 1).then_inc(S.selok, 1)
+
+    v.wait_ge(S.ldtab, 32)
+    v.tensor_copy(T.tabb[:], T.tab[:]).then_inc(S.cv, 1)
+    pe.wait_ge(S.selok, 1)
+    pe.wait_ge(S.cv, 1)
+    pe.matmul(offp[:, 0:4], T.sel[:], T.tabb[:], True, True).then_inc(S.mmoff, 1)
+    v.wait_ge(S.mmoff, 1)
+    v.tensor_copy(T.off[:], offp[:, 0:4]).then_inc(S.offok, 1)
+    v.wait_ge(S.offok, 1)
+    v.wait_ge(S.ldx, 16)
+    v.wait_ge(S.msslots, 1)
+    v.tensor_copy(T.slots[:, 0:WIN].indirect(T.off[:, 0:4]), T.xs[:, 0:TOK]).then_inc(S.sc, 1)
+    v.wait_ge(S.sc, 1)
+    oc = groups[OWN_GROUP]["own"]
+    v.tensor_copy(T.xin[:, oc:oc + CAP], T.slots[:, mine:mine + CAP]).then_inc(S.owncp, 1)
+
+    g.wait_ge(S.sc, 1)
+    sent = 0
+    for gi, grp in enumerate(groups):
+        items = []
+        for d, ne, col in grp["mem"]:
+            k = (me + d) % N
+            items.append((cores[k], ne, T.slots[:, k * STRIDE:k * STRIDE + CAP], T.xin[:, col:col + CAP],
+                          S["arr%d" % gi]))
+            sent += ne
+        send(g, core, topo, items, S.lsem)
+
+    pe.wait_ge(S.ldw1, 16)
+    for gi, grp in enumerate(groups):
+        c0, n = grp["c0"], grp["n"]
+        pe.wait_ge(S["arr%d" % gi], sum(ne for d, ne, col in grp["mem"]))
+        if grp["own"] is not None:
+            pe.wait_ge(S.owncp, 1)
+        for t in range(FF + AHEAD):
+            if t < FF:
+                pe.matmul(hbank[t % HB][:, 0:n], T.w1s[:, t * D:(t + 1) * D], T.xin[:, c0:c0 + n], True, True
+                          ).then_inc(S["l1_%d_%d" % (gi, t)], 1)
+                h = T.hs[:, t * COLS + c0:t * COLS + c0 + n]
+                if t % 2 == 0:
+                    v.wait_ge(S["l1_%d_%d" % (gi, t)], 1)
+                    v.tensor_scalar(h, hbank[t % HB][:, 0:n], 0.0, None, AluOpType.max
+                                    ).then_inc(S["rl_%d_%d" % (gi, t)], 1)
+                else:
+                    act.wait_ge(S["l1_%d_%d" % (gi, t)], 1)
+                    act.activation(h, hbank[t % HB][:, 0:n], ActivationFunctionType.Relu
+                                   ).then_inc(S["rl_%d_%d" % (gi, t)], 1)
+            f = t - AHEAD
+            if f >= 0:
+                if gi == 0 and f == 0:
+                    pe.wait_ge(S.ldw2, 16)
+                pe.wait_ge(S["rl_%d_%d" % (gi, f)], 1)
+                mm = pe.matmul(ybank[gi][:, 0:n], T.w2s[:, f * D:(f + 1) * D],
+                               T.hs[:, f * COLS + c0:f * COLS + c0 + n], f == 0, f == FF - 1)
+                if f == FF - 1:
+                    mm.then_inc(S["l2_%d" % gi], 1)
+        r0 = grp["mem"][0][2]
+        v.wait_ge(S["l2_%d" % gi], 1)
+        v.tensor_copy(T.yo[:, r0:c0 + n], ybank[gi][:, r0 - c0:n]).then_inc(S["ev%d" % gi], 1)
+        if grp["own"] is not None:
+            v.tensor_copy(T.back[:, mine:mine + CAP], ybank[gi][:, 0:CAP]).then_inc(S.evown, 1)
+        g.wait_ge(S["ev%d" % gi], 1)
+        items = []
+        for d, ne, col in grp["mem"]:
+            items.append((cores[(me - d) % N], ne, T.yo[:, col:col + CAP], T.back[:, mine:mine + CAP], S.ret))
+            sent += ne
+        send(g, core, topo, items, S.lsem)
+
+    v.wait_ge(S.ret, sum(ne for grp in groups for d, ne, col in grp["mem"]))
+    v.wait_ge(S.evown, 1)
+    v.wait_ge(S.msback, N)
+    v.tensor_copy(T.ys[:, 0:TOK], T.back[:, 0:WIN].indirect(T.off[:, 0:4])).then_inc(S.gat, 1)
+    sy.wait_ge(S.gat, 1)
+    sy.dma_start(T.y[:], T.ys[:]).then_inc(S.st, 16)
+    sy.wait_ge(S.st, 16)
+    g.wait_ge(S.lsem, sent)

@@ -5,9 +5,10 @@ N, TOK, CAP, FF, D = 6, 64, 32, 8, 128
 STRIDE = 2 * CAP
 WIN = N * STRIDE
 WAVES = [[8], [4, 4], [4, 4]]
-OWN_GROUP = 0
 NG = len(WAVES)
-COLS = N * CAP
+OWN = NG
+COLS = TOK + 4 * CAP
+HCOLS = COLS + CAP
 HB, AHEAD = 4, 3
 
 SCRATCH = {
@@ -20,18 +21,20 @@ SCRATCH = {
     "xin": ("sbuf", [D, COLS], "bfloat16"),
     "w1s": ("sbuf", [D, FF * D], "bfloat16"),
     "w2s": ("sbuf", [D, FF * D], "bfloat16"),
-    "hs": ("sbuf", [D, FF * COLS], "bfloat16"),
+    "hs": ("sbuf", [D, FF * HCOLS], "bfloat16"),
     "yo": ("sbuf", [D, COLS], "bfloat16"),
+    "rd": ("sbuf", [D, TOK], "bfloat16"),
+    "win2": ("sbuf", [D, WIN], "bfloat16"),
     "back": ("sbuf", [D, WIN], "bfloat16"),
     "ys": ("sbuf", [D, TOK], "bfloat16"),
 }
 for _b in range(8):
     SCRATCH["p%d" % _b] = ("psum", [D, 512], "float32")
 
-SEMAPHORES = ["ldtab", "ldx", "ldw1", "ldw2", "mssel", "sel1", "selok", "msslots", "msback", "cv", "mmoff", "offok",
-              "sc", "owncp", "evown", "ret", "gat", "st", "lsem"]
-for _g in range(NG):
-    SEMAPHORES += ["arr%d" % _g, "l2_%d" % _g, "ev%d" % _g]
+SEMAPHORES = ["ldtab", "ldx", "ldw1", "ldw2", "mssel", "sel1", "selok", "msslots", "msback", "mswin2", "cv", "mmoff",
+              "offok", "sc", "ret", "retd", "sc2", "cp2", "gat", "st", "lsem"]
+for _g in range(NG + 1):
+    SEMAPHORES += ["arr%d" % _g, "l2_%d" % _g, "ev%d" % _g][(1 if _g == OWN else 0):]
     for _f in range(FF):
         SEMAPHORES += ["l1_%d_%d" % (_g, _f), "rl_%d_%d" % (_g, _f)]
 
@@ -50,16 +53,13 @@ def plan(cores, topo):
     order = sorted(range(1, n), key=lambda d: (-hops(d), d))
     groups, i, col = [], 0, 0
     for gi, shape in enumerate(WAVES):
-        c0, own = col, None
-        if gi == OWN_GROUP:
-            own = col
-            col += CAP
         mem = []
         for ne in shape:
-            mem.append((order[i], ne, col))
+            w = TOK if gi == 0 else CAP
+            mem.append((order[i], ne, col, w))
             i += 1
-            col += CAP
-        groups.append({"c0": c0, "n": col - c0, "own": own, "mem": mem})
+            col += w
+        groups.append(mem)
     return groups
 
 
@@ -94,12 +94,15 @@ def rank_program(g, core, T, topo):
     groups = plan(cores, topo)
     mine = me * STRIDE
     hbank = [T["p%d" % b] for b in range(HB)]
-    ybank = [T["p%d" % (HB + gi)] for gi in range(NG)]
-    offp = T.p7
+    ybank = [T["p%d" % (HB + gi)] for gi in range(NG + 1)]
+    offp = ybank[OWN]
+    d0 = groups[0][0][0]
+    k0 = ((me + d0) % N) * STRIDE
+    sent = 0
 
-    sy.dma_start(T.tab[0:16, :], T.ex[:]).then_inc(S.ldtab, 16)
-    act.dma_start(T.tab[16:32, :], T.pos[:]).then_inc(S.ldtab, 16)
     sy.dma_start(T.xs[:], T.x[:]).then_inc(S.ldx, 16)
+    act.dma_start(T.tab[0:16, :], T.ex[:]).then_inc(S.ldtab, 16)
+    sy.dma_start(T.tab[16:32, :], T.pos[:]).then_inc(S.ldtab, 16)
     sy.dma_start(T.w1s[:], T.w1[:]).then_inc(S.ldw1, 16)
     sy.dma_start(T.w2s[:], T.w2[:]).then_inc(S.ldw2, 16)
 
@@ -107,10 +110,16 @@ def rank_program(g, core, T, topo):
     v.memset(T.slots[:], 0.0).then_inc(S.msslots, 1)
     for k in range(N):
         v.memset(T.back[:, k * STRIDE + CAP:(k + 1) * STRIDE], 0.0).then_inc(S.msback, 1)
+    v.memset(T.win2[:, k0:k0 + CAP], 0.0).then_inc(S.mswin2, 1)
     g.wait_ge(S.mssel, 1)
     g.affine_select(T.sel[:], T.sel[:], [[0, D // 16], [-1, 16]], AluOpType.is_equal, 0.0, 0, 1).then_inc(S.sel1, 1)
     g.wait_ge(S.sel1, 1)
     g.affine_select(T.sel[:], T.sel[:], [[0, D // 16], [-1, 16]], AluOpType.not_equal, 1.0, -16, 1).then_inc(S.selok, 1)
+
+    g.wait_ge(S.ldx, 16)
+    d, ne, col, w = groups[0][0]
+    send(g, core, topo, [(cores[(me + d) % N], ne, T.xs[:, 0:TOK], T.xin[:, col:col + w], S.arr0)], S.lsem)
+    sent += ne
 
     v.wait_ge(S.ldtab, 32)
     v.tensor_copy(T.tabb[:], T.tab[:]).then_inc(S.cv, 1)
@@ -123,63 +132,73 @@ def rank_program(g, core, T, topo):
     v.wait_ge(S.ldx, 16)
     v.wait_ge(S.msslots, 1)
     v.tensor_copy(T.slots[:, 0:WIN].indirect(T.off[:, 0:4]), T.xs[:, 0:TOK]).then_inc(S.sc, 1)
-    v.wait_ge(S.sc, 1)
-    oc = groups[OWN_GROUP]["own"]
-    v.tensor_copy(T.xin[:, oc:oc + CAP], T.slots[:, mine:mine + CAP]).then_inc(S.owncp, 1)
 
     g.wait_ge(S.sc, 1)
-    sent = 0
-    for gi, grp in enumerate(groups):
+    for gi in range(1, NG):
         items = []
-        for d, ne, col in grp["mem"]:
+        for d, ne, col, w in groups[gi]:
             k = (me + d) % N
-            items.append((cores[k], ne, T.slots[:, k * STRIDE:k * STRIDE + CAP], T.xin[:, col:col + CAP],
+            items.append((cores[k], ne, T.slots[:, k * STRIDE:k * STRIDE + CAP], T.xin[:, col:col + w],
                           S["arr%d" % gi]))
             sent += ne
         send(g, core, topo, items, S.lsem)
 
-    pe.wait_ge(S.ldw1, 16)
-    for gi, grp in enumerate(groups):
-        c0, n = grp["c0"], grp["n"]
-        pe.wait_ge(S["arr%d" % gi], sum(ne for d, ne, col in grp["mem"]))
-        if grp["own"] is not None:
-            pe.wait_ge(S.owncp, 1)
+    def ffn(gi, rhs, n, hcol, both):
         for t in range(FF + AHEAD):
             if t < FF:
-                pe.matmul(hbank[t % HB][:, 0:n], T.w1s[:, t * D:(t + 1) * D], T.xin[:, c0:c0 + n], True, True
-                          ).then_inc(S["l1_%d_%d" % (gi, t)], 1)
-                h = T.hs[:, t * COLS + c0:t * COLS + c0 + n]
-                if t % 2 == 0:
-                    v.wait_ge(S["l1_%d_%d" % (gi, t)], 1)
-                    v.tensor_scalar(h, hbank[t % HB][:, 0:n], 0.0, None, AluOpType.max
-                                    ).then_inc(S["rl_%d_%d" % (gi, t)], 1)
+                l1, rl = S["l1_%d_%d" % (gi, t)], S["rl_%d_%d" % (gi, t)]
+                pe.matmul(hbank[t % HB][:, 0:n], T.w1s[:, t * D:(t + 1) * D], rhs, True, True).then_inc(l1, 1)
+                h = T.hs[:, t * HCOLS + hcol:t * HCOLS + hcol + n]
+                if both and t % 2 == 0:
+                    v.wait_ge(l1, 1)
+                    v.tensor_scalar(h, hbank[t % HB][:, 0:n], 0.0, None, AluOpType.max).then_inc(rl, 1)
                 else:
-                    act.wait_ge(S["l1_%d_%d" % (gi, t)], 1)
-                    act.activation(h, hbank[t % HB][:, 0:n], ActivationFunctionType.Relu
-                                   ).then_inc(S["rl_%d_%d" % (gi, t)], 1)
+                    act.wait_ge(l1, 1)
+                    act.activation(h, hbank[t % HB][:, 0:n], ActivationFunctionType.Relu).then_inc(rl, 1)
             f = t - AHEAD
             if f >= 0:
                 if gi == 0 and f == 0:
                     pe.wait_ge(S.ldw2, 16)
                 pe.wait_ge(S["rl_%d_%d" % (gi, f)], 1)
                 mm = pe.matmul(ybank[gi][:, 0:n], T.w2s[:, f * D:(f + 1) * D],
-                               T.hs[:, f * COLS + c0:f * COLS + c0 + n], f == 0, f == FF - 1)
+                               T.hs[:, f * HCOLS + hcol:f * HCOLS + hcol + n], f == 0, f == FF - 1)
                 if f == FF - 1:
                     mm.then_inc(S["l2_%d" % gi], 1)
-        r0 = grp["mem"][0][2]
+
+    pe.wait_ge(S.ldw1, 16)
+    for gi, mem in enumerate(groups):
+        c0 = mem[0][2]
+        n = sum(w for d, ne, col, w in mem)
+        pe.wait_ge(S["arr%d" % gi], sum(ne for d, ne, col, w in mem))
+        ffn(gi, T.xin[:, c0:c0 + n], n, c0, True)
         v.wait_ge(S["l2_%d" % gi], 1)
-        v.tensor_copy(T.yo[:, r0:c0 + n], ybank[gi][:, r0 - c0:n]).then_inc(S["ev%d" % gi], 1)
-        if grp["own"] is not None:
-            v.tensor_copy(T.back[:, mine:mine + CAP], ybank[gi][:, 0:CAP]).then_inc(S.evown, 1)
+        v.tensor_copy(T.yo[:, c0:c0 + n], ybank[gi][:, 0:n]).then_inc(S["ev%d" % gi], 1)
         g.wait_ge(S["ev%d" % gi], 1)
         items = []
-        for d, ne, col in grp["mem"]:
-            items.append((cores[(me - d) % N], ne, T.yo[:, col:col + CAP], T.back[:, mine:mine + CAP], S.ret))
+        for d, ne, col, w in mem:
+            if gi == 0:
+                items.append((cores[(me - d) % N], ne, T.yo[:, col:col + w], T.rd[:, 0:TOK], S.retd))
+            else:
+                items.append((cores[(me - d) % N], ne, T.yo[:, col:col + w], T.back[:, mine:mine + CAP], S.ret))
             sent += ne
         send(g, core, topo, items, S.lsem)
 
-    v.wait_ge(S.ret, sum(ne for grp in groups for d, ne, col in grp["mem"]))
-    v.wait_ge(S.evown, 1)
+    pe.wait_ge(S.sc, 1)
+    pe.wait_ge(S.offok, 1)
+    ffn(OWN, T.slots[:, mine:mine + CAP], CAP, COLS, False)
+    act.wait_ge(S["l2_%d" % OWN], 1)
+    act.activation(T.back[:, mine:mine + CAP], ybank[OWN][:, 0:CAP], ActivationFunctionType.Copy
+                   ).then_inc(S["ev%d" % OWN], 1)
+
+    v.wait_ge(S.retd, groups[0][0][1])
+    v.wait_ge(S.mswin2, 1)
+    v.tensor_copy(T.win2[:, 0:WIN].indirect(T.off[:, 0:4]), T.rd[:, 0:TOK]).then_inc(S.sc2, 1)
+    v.wait_ge(S.sc2, 1)
+    v.tensor_copy(T.back[:, k0:k0 + CAP], T.win2[:, k0:k0 + CAP]).then_inc(S.cp2, 1)
+
+    v.wait_ge(S.cp2, 1)
+    v.wait_ge(S.ret, sum(ne for mem in groups[1:] for d, ne, col, w in mem))
+    v.wait_ge(S["ev%d" % OWN], 1)
     v.wait_ge(S.msback, N)
     v.tensor_copy(T.ys[:, 0:TOK], T.back[:, 0:WIN].indirect(T.off[:, 0:4])).then_inc(S.gat, 1)
     sy.wait_ge(S.gat, 1)

@@ -9,7 +9,8 @@ NG = len(WAVES)
 OWN = NG
 COLS = TOK + 4 * CAP
 HCOLS = COLS + CAP
-HB, AHEAD = 4, 3
+BANKS = [(0, 1), (2, 3), (4, 5), (6,), (7,)]
+HB, YB = len(BANKS), 8 - len(BANKS)
 
 SCRATCH = {
     "tab": ("sbuf", [32, 4], "int32"),
@@ -35,7 +36,7 @@ SEMAPHORES = ["ldtab", "ldx", "ldw1", "ldw2", "mssel", "sel1", "selok", "msslots
               "offok", "sc", "ret", "retd", "sc2", "cp2", "gat", "st", "lsem"]
 for _g in range(NG + 1):
     SEMAPHORES += ["arr%d" % _g, "l2_%d" % _g, "ev%d" % _g][(1 if _g == OWN else 0):]
-    for _f in range(FF):
+    for _f in range(HB):
         SEMAPHORES += ["l1_%d_%d" % (_g, _f), "rl_%d_%d" % (_g, _f)]
 
 
@@ -94,8 +95,8 @@ def rank_program(g, core, T, topo):
     groups = plan(cores, topo)
     mine = me * STRIDE
     hbank = [T["p%d" % b] for b in range(HB)]
-    ybank = [T["p%d" % (HB + gi)] for gi in range(NG + 1)]
-    offp = ybank[OWN]
+    ybank = [T["p%d" % (HB + gi % YB)] for gi in range(NG + 1)]
+    offp = ybank[NG - 1]
     d0 = groups[0][0][0]
     k0 = ((me + d0) % N) * STRIDE
     sent = 0
@@ -144,28 +145,31 @@ def rank_program(g, core, T, topo):
         send(g, core, topo, items, S.lsem)
 
     def ffn(gi, rhs, n, hcol, both):
-        for t in range(FF + AHEAD):
-            if t < FF:
-                l1, rl = S["l1_%d_%d" % (gi, t)], S["rl_%d_%d" % (gi, t)]
-                pe.matmul(hbank[t % HB][:, 0:n], T.w1s[:, t * D:(t + 1) * D], rhs, True, True).then_inc(l1, 1)
-                h = T.hs[:, t * HCOLS + hcol:t * HCOLS + hcol + n]
-                if both and t % 2 == 0:
-                    v.wait_ge(l1, 1)
-                    v.tensor_scalar(h, hbank[t % HB][:, 0:n], 0.0, None, AluOpType.max).then_inc(rl, 1)
-                else:
-                    act.wait_ge(l1, 1)
-                    act.activation(h, hbank[t % HB][:, 0:n], ActivationFunctionType.Relu).then_inc(rl, 1)
-            f = t - AHEAD
-            if f >= 0:
-                if gi == 0 and f == 0:
-                    pe.wait_ge(S.ldw2, 16)
-                pe.wait_ge(S["rl_%d_%d" % (gi, f)], 1)
-                mm = pe.matmul(ybank[gi][:, 0:n], T.w2s[:, f * D:(f + 1) * D],
-                               T.hs[:, f * HCOLS + hcol:f * HCOLS + hcol + n], f == 0, f == FF - 1)
+        base = FF * hcol
+        for b, tiles in enumerate(BANKS):
+            l1, rl = S["l1_%d_%d" % (gi, b)], S["rl_%d_%d" % (gi, b)]
+            for j, t in enumerate(tiles):
+                pe.matmul(hbank[b][:, j * n:(j + 1) * n], T.w1s[:, t * D:(t + 1) * D], rhs, True, True).then_inc(l1, 1)
+            m = len(tiles) * n
+            h = T.hs[:, base + tiles[0] * n:base + tiles[0] * n + m]
+            if both and b % 2 == 0:
+                v.wait_ge(l1, len(tiles))
+                v.tensor_scalar(h, hbank[b][:, 0:m], 0.0, None, AluOpType.max).then_inc(rl, 1)
+            else:
+                act.wait_ge(l1, len(tiles))
+                act.activation(h, hbank[b][:, 0:m], ActivationFunctionType.Relu).then_inc(rl, 1)
+        if gi == 0:
+            pe.wait_ge(S.ldw2, 16)
+        for b, tiles in enumerate(BANKS):
+            pe.wait_ge(S["rl_%d_%d" % (gi, b)], 1)
+            for f in tiles:
+                mm = pe.matmul(ybank[gi][:, 0:n], T.w2s[:, f * D:(f + 1) * D], T.hs[:, base + f * n:base + (f + 1) * n],
+                               f == 0, f == FF - 1)
                 if f == FF - 1:
                     mm.then_inc(S["l2_%d" % gi], 1)
 
     pe.wait_ge(S.ldw1, 16)
+    pe.wait_ge(S.offok, 1)
     for gi, mem in enumerate(groups):
         c0 = mem[0][2]
         n = sum(w for d, ne, col, w in mem)
@@ -184,7 +188,7 @@ def rank_program(g, core, T, topo):
         send(g, core, topo, items, S.lsem)
 
     pe.wait_ge(S.sc, 1)
-    pe.wait_ge(S.offok, 1)
+    pe.wait_ge(S.ev0, 1)
     ffn(OWN, T.slots[:, mine:mine + CAP], CAP, COLS, False)
     act.wait_ge(S["l2_%d" % OWN], 1)
     act.activation(T.back[:, mine:mine + CAP], ybank[OWN][:, 0:CAP], ActivationFunctionType.Copy

from concourse.bass import DstId, RemoteDMATransfer
from concourse.mybir import AluOpType, ActivationFunctionType

N, TOK, CAP, FF, D = 6, 64, 32, 8, 128
STRIDE = 2 * CAP
WIN = N * STRIDE
WAVES = [[8], [4, 4], [4, 4]]
NG = len(WAVES)
OWN = NG
COLS = TOK + 4 * CAP
HCOLS = COLS + CAP
BANKS = [(0, 1), (2, 3), (4, 5), (6,), (7,)]
HB, YB = len(BANKS), 8 - len(BANKS)

SCRATCH = {
    "tab": ("sbuf", [32, 4], "int32"),
    "tabb": ("sbuf", [32, 4], "bfloat16"),
    "sel": ("sbuf", [32, D], "bfloat16"),
    "off": ("sbuf", [D, 4], "uint16"),
    "xs": ("sbuf", [D, TOK], "bfloat16"),
    "slots": ("sbuf", [D, WIN], "bfloat16"),
    "xin": ("sbuf", [D, COLS], "bfloat16"),
    "w1s": ("sbuf", [D, FF * D], "bfloat16"),
    "w2s": ("sbuf", [D, FF * D], "bfloat16"),
    "hs": ("sbuf", [D, FF * HCOLS], "bfloat16"),
    "yo": ("sbuf", [D, COLS], "bfloat16"),
    "rd": ("sbuf", [D, TOK], "bfloat16"),
    "win2": ("sbuf", [D, WIN], "bfloat16"),
    "back": ("sbuf", [D, WIN], "bfloat16"),
    "ys": ("sbuf", [D, TOK], "bfloat16"),
}
for _b in range(8):
    SCRATCH["p%d" % _b] = ("psum", [D, 512], "float32")

SEMAPHORES = ["ldtab", "ldx", "ldw1", "ldw2", "mssel", "sel1", "selok", "msslots", "msback", "mswin2", "cv", "mmoff",
              "offok", "sc", "ret", "retd", "sc2", "cp2", "gat", "st", "lsem"]
for _g in range(NG + 1):
    SEMAPHORES += ["arr%d" % _g, "l2_%d" % _g, "ev%d" % _g][(1 if _g == OWN else 0):]
    for _f in range(HB):
        SEMAPHORES += ["l1_%d_%d" % (_g, _f), "rl_%d_%d" % (_g, _f)]


def plan(cores, topo):
    n = len(cores)

    def hops(d):
        worst = 1
        for r in range(n):
            a, b = topo.chip(cores[r]), topo.chip(cores[(r + d) % n])
            if not (topo.mates(a, b) or topo.same_plane(a, b)):
                worst = 2
        return worst

    order = sorted(range(1, n), key=lambda d: (-hops(d), d))
    groups, i, col = [], 0, 0
    for gi, shape in enumerate(WAVES):
        mem = []
        for ne in shape:
            w = TOK if gi == 0 else CAP
            mem.append((order[i], ne, col, w))
            i += 1
            col += w
        groups.append(mem)
    return groups


def send(g, core, topo, items, local_sem):
    used, trs = 0, []
    for dst, ne, src, land, rsem in items:
        if not topo.may_write(core, dst):
            raise ValueError("no way from %d to %d" % (core, dst))
        allowed = topo.mask(core, dst)
        free = [b for b in range(allowed.bit_length()) if (allowed >> b) & 1 and not (used >> b) & 1]
        m = 0
        for b in free[:ne]:
            m |= 1 << b
        used |= m
        rid, pid, ring = topo.addr(dst)
        trs.append((rid, pid, m, src, land, rsem))
    if len(trs) == 1:
        rid, pid, m, src, land, rsem = trs[0]
        g.remote_dma(land, src, rsem, local_sem, pid, rid, m)
    else:
        g.remote_dma_fused([RemoteDMATransfer(dst_ids=[DstId(rid=rid, pnc=pid)], dma_engine_mask=m, remote_sem=rsem,
                                              src=src, dst=land) for rid, pid, m, src, land, rsem in trs],
                           local_sem=local_sem)


def rank_program(g, core, T, topo):
    me = T.rank_of(core)
    if me is None:
        return
    S, cores = T.sem, T.cores
    v, pe, act, sy = g.vector, g.tensor, g.scalar, g.sync
    groups = plan(cores, topo)
    mine = me * STRIDE
    hbank = [T["p%d" % b] for b in range(HB)]
    ybank = [T["p%d" % (HB + gi % YB)] for gi in range(NG + 1)]
    offp = ybank[NG - 1]
    d0 = groups[0][0][0]
    k0 = ((me + d0) % N) * STRIDE
    sent = 0

    sy.dma_start(T.xs[:], T.x[:]).then_inc(S.ldx, 16)
    act.dma_start(T.tab[0:16, :], T.ex[:]).then_inc(S.ldtab, 16)
    sy.dma_start(T.tab[16:32, :], T.pos[:]).then_inc(S.ldtab, 16)
    sy.dma_start(T.w1s[:], T.w1[:]).then_inc(S.ldw1, 16)
    sy.dma_start(T.w2s[:], T.w2[:]).then_inc(S.ldw2, 16)

    v.memset(T.sel[:], 64.0).then_inc(S.mssel, 1)
    v.memset(T.slots[:], 0.0).then_inc(S.msslots, 1)
    for k in range(N):
        v.memset(T.back[:, k * STRIDE + CAP:(k + 1) * STRIDE], 0.0).then_inc(S.msback, 1)
    v.memset(T.win2[:, k0:k0 + CAP], 0.0).then_inc(S.mswin2, 1)
    g.wait_ge(S.mssel, 1)
    g.affine_select(T.sel[:], T.sel[:], [[0, D // 16], [-1, 16]], AluOpType.is_equal, 0.0, 0, 1).then_inc(S.sel1, 1)
    g.wait_ge(S.sel1, 1)
    g.affine_select(T.sel[:], T.sel[:], [[0, D // 16], [-1, 16]], AluOpType.not_equal, 1.0, -16, 1).then_inc(S.selok, 1)

    g.wait_ge(S.ldx, 16)
    d, ne, col, w = groups[0][0]
    send(g, core, topo, [(cores[(me + d) % N], ne, T.xs[:, 0:TOK], T.xin[:, col:col + w], S.arr0)], S.lsem)
    sent += ne

    v.wait_ge(S.ldtab, 32)
    v.tensor_copy(T.tabb[:], T.tab[:]).then_inc(S.cv, 1)
    pe.wait_ge(S.selok, 1)
    pe.wait_ge(S.cv, 1)
    pe.matmul(offp[:, 0:4], T.sel[:], T.tabb[:], True, True).then_inc(S.mmoff, 1)
    v.wait_ge(S.mmoff, 1)
    v.tensor_copy(T.off[:], offp[:, 0:4]).then_inc(S.offok, 1)
    v.wait_ge(S.offok, 1)
    v.wait_ge(S.ldx, 16)
    v.wait_ge(S.msslots, 1)
    v.tensor_copy(T.slots[:, 0:WIN].indirect(T.off[:, 0:4]), T.xs[:, 0:TOK]).then_inc(S.sc, 1)

    g.wait_ge(S.sc, 1)
    for gi in range(1, NG):
        items = []
        for d, ne, col, w in groups[gi]:
            k = (me + d) % N
            items.append((cores[k], ne, T.slots[:, k * STRIDE:k * STRIDE + CAP], T.xin[:, col:col + w],
                          S["arr%d" % gi]))
            sent += ne
        send(g, core, topo, items, S.lsem)

    def ffn(gi, rhs, n, hcol, both):
        base = FF * hcol
        for b, tiles in enumerate(BANKS):
            l1, rl = S["l1_%d_%d" % (gi, b)], S["rl_%d_%d" % (gi, b)]
            for j, t in enumerate(tiles):
                pe.matmul(hbank[b][:, j * n:(j + 1) * n], T.w1s[:, t * D:(t + 1) * D], rhs, True, True).then_inc(l1, 1)
            m = len(tiles) * n
            h = T.hs[:, base + tiles[0] * n:base + tiles[0] * n + m]
            if both and b % 2 == 0:
                v.wait_ge(l1, len(tiles))
                v.tensor_scalar(h, hbank[b][:, 0:m], 0.0, None, AluOpType.max).then_inc(rl, 1)
            else:
                act.wait_ge(l1, len(tiles))
                act.activation(h, hbank[b][:, 0:m], ActivationFunctionType.Relu).then_inc(rl, 1)
        if gi == 0:
            pe.wait_ge(S.ldw2, 16)
        for b, tiles in enumerate(BANKS):
            pe.wait_ge(S["rl_%d_%d" % (gi, b)], 1)
            for f in tiles:
                mm = pe.matmul(ybank[gi][:, 0:n], T.w2s[:, f * D:(f + 1) * D], T.hs[:, base + f * n:base + (f + 1) * n],
                               f == 0, f == FF - 1)
                if f == FF - 1:
                    mm.then_inc(S["l2_%d" % gi], 1)

    pe.wait_ge(S.ldw1, 16)
    pe.wait_ge(S.offok, 1)
    for gi, mem in enumerate(groups):
        c0 = mem[0][2]
        n = sum(w for d, ne, col, w in mem)
        pe.wait_ge(S["arr%d" % gi], sum(ne for d, ne, col, w in mem))
        ffn(gi, T.xin[:, c0:c0 + n], n, c0, True)
        v.wait_ge(S["l2_%d" % gi], 1)
        v.tensor_copy(T.yo[:, c0:c0 + n], ybank[gi][:, 0:n]).then_inc(S["ev%d" % gi], 1)
        g.wait_ge(S["ev%d" % gi], 1)
        items = []
        for d, ne, col, w in mem:
            if gi == 0:
                items.append((cores[(me - d) % N], ne, T.yo[:, col:col + w], T.rd[:, 0:TOK], S.retd))
            else:
                items.append((cores[(me - d) % N], ne, T.yo[:, col:col + w], T.back[:, mine:mine + CAP], S.ret))
            sent += ne
        send(g, core, topo, items, S.lsem)

    pe.wait_ge(S.sc, 1)
    pe.wait_ge(S.ev0, 1)
    ffn(OWN, T.slots[:, mine:mine + CAP], CAP, COLS, False)
    act.wait_ge(S["l2_%d" % OWN], 1)
    act.activation(T.back[:, mine:mine + CAP], ybank[OWN][:, 0:CAP], ActivationFunctionType.Copy
                   ).then_inc(S["ev%d" % OWN], 1)

    v.wait_ge(S.retd, groups[0][0][1])
    v.wait_ge(S.mswin2, 1)
    v.tensor_copy(T.win2[:, 0:WIN].indirect(T.off[:, 0:4]), T.rd[:, 0:TOK]).then_inc(S.sc2, 1)
    v.wait_ge(S.sc2, 1)
    v.tensor_copy(T.back[:, k0:k0 + CAP], T.win2[:, k0:k0 + CAP]).then_inc(S.cp2, 1)

    v.wait_ge(S.cp2, 1)
    v.wait_ge(S.ret, sum(ne for mem in groups[1:] for d, ne, col, w in mem))
    v.wait_ge(S["ev%d" % OWN], 1)
    v.wait_ge(S.msback, N)
    v.tensor_copy(T.ys[:, 0:TOK], T.back[:, 0:WIN].indirect(T.off[:, 0:4])).then_inc(S.gat, 1)
    sy.wait_ge(S.gat, 1)
    sy.dma_start(T.y[:], T.ys[:]).then_inc(S.st, 16)
    sy.wait_ge(S.st, 16)
    g.wait_ge(S.lsem, sent)
